import numpy as np
CORES = [2,6,10,14]
N = 4
def setup_inputs(rng):
    return {"x1": rng.standard_normal((N, 128, 256), dtype=np.float32), "x2": rng.standard_normal((N, 128, 1), dtype=np.float32), "x3": rng.standard_normal((N, 128, 1024), dtype=np.float32), "x4": rng.standard_normal((N, 128, 64), dtype=np.float32)}
def reference(x1, x2, x3, x4):
    out = {}
    s = x1.sum(axis=0, dtype=np.float64).astype(x1.dtype)
    out["y1"] = np.broadcast_to(s, (N,) + s.shape)
    s = x2.sum(axis=0, dtype=np.float64).astype(x2.dtype)
    out["y2"] = np.broadcast_to(s, (N,) + s.shape)
    s = x3.sum(axis=0, dtype=np.float64).astype(x3.dtype)
    out["y3"] = np.broadcast_to(s, (N,) + s.shape)
    s = x4.sum(axis=0, dtype=np.float64).astype(x4.dtype)
    out["y4"] = np.broadcast_to(s, (N,) + s.shape)
    return out

@@ -1,0 +1,100 @@
+from concourse.bass import DstId, RemoteDMATransfer
+
+W3 = 2
+N3 = 256 // W3
+NS = 32
+KS = 11
+RED = [3, 7, 11, 15]
+JS = 3
+
+SCRATCH = {
+    "p3": ("dram", [4 * W3, 128, N3], "float32"),
+    "ps": ("dram", [KS, 128, NS], "float32"),
+    "r3": ("dram", [4 * W3, 128, N3], "float32"),
+    "rs": ("dram", [4 * JS, 128, NS], "float32"),
+    "l3": ("dram", [4 * W3, 128, N3], "float32"),
+    "ls": ("dram", [KS, 128, NS], "float32"),
+}
+SEMAPHORES = (["lds", "arrs", "sums", "sent", "st"]
+              + ["ld3_%d" % w for w in range(W3)] + ["arr3_%d" % w for w in range(W3)]
+              + ["sum3_%d" % w for w in range(W3)])
+
+
+def bits(first, count):
+    return ((1 << count) - 1) << first
+
+
+def dst_id(topo, c):
+    rid, pid, _ = topo.addr(c)
+    return DstId(rid=rid, pnc=pid)
+
+
+def send(g, T, topo, core, items, per, sem):
+    nxt = {True: 0, False: 8}
+    trs = []
+    for src, red, dst in items:
+        off = topo.chip(red) != topo.chip(core)
+        trs.append(RemoteDMATransfer(dst_ids=[dst_id(topo, red)], dma_engine_mask=bits(nxt[off], per),
+                                     remote_sem=sem, src=src, dst=dst))
+        nxt[off] += per
+    g.remote_dma_fused(trs, local_sem=T.sem.sent)
+    return per * len(trs)
+
+
+def fold(g, T, topo, core, items, per, sem):
+    far = [c for c in T.cores if topo.chip(c) != topo.chip(core)]
+    near = [c for c in T.cores if topo.chip(c) == topo.chip(core)]
+    trs = []
+    for i, (srcs, dst) in enumerate(items):
+        for base, group in ((0, far), (8, near)):
+            trs.append(RemoteDMATransfer(dst_ids=[dst_id(topo, c) for c in group],
+                                         dma_engine_mask=bits(base + i * per, per), remote_sem=sem,
+                                         srcs=srcs, dsts=[dst for c in group], alu_op=1))
+    g.remote_dma_fused(trs, local_sem=T.sem.sent)
+    return per * len(trs)
+
+
+def run_rank(g, core, T, topo, rank):
+    rows = 128 // W3
+    g.scalar.dma_start(T.ps[0:8], T.x1[:]).then_inc(T.sem.lds, 16)
+    g.scalar.dma_start(T.ps[8:10], T.x4[:]).then_inc(T.sem.lds, 16)
+    g.scalar.dma_start(T.ps[10, 0:4, :], T.x2[:, 0]).then_inc(T.sem.lds, 16)
+    g.scalar.dma_start(T.ps[10, 4:128, :], T.x4[0:62, :]).then_inc(T.sem.lds, 16)
+    for w in range(W3):
+        g.sync.dma_start(T.p3[4 * w:4 * w + 4], T.x3[w * rows:(w + 1) * rows, :]).then_inc(T.sem["ld3_%d" % w], 16)
+    g.wait_ge(T.sem.lds, 64)
+    sent = send(g, T, topo, core, [(T.ps[j], RED[j % 4], T.rs[rank * JS + j // 4]) for j in range(KS)], 1, T.sem.arrs)
+    for w in range(W3):
+        g.wait_ge(T.sem["ld3_%d" % w], 16)
+        sent += send(g, T, topo, core, [(T.p3[4 * w + k], RED[k], T.r3[rank * W3 + w]) for k in range(4)], 4,
+                     T.sem["arr3_%d" % w])
+    g.scalar.wait_ge(T.sem.sums, 2 * KS)
+    g.scalar.dma_start(T.y1[:], T.ls[0:8]).then_inc(T.sem.st, 16)
+    g.scalar.dma_start(T.y4[:], T.ls[8:10]).then_inc(T.sem.st, 16)
+    g.scalar.dma_start(T.y2[:, 0], T.ls[10, 0:4, :]).then_inc(T.sem.st, 16)
+    for w in range(W3):
+        g.sync.wait_ge(T.sem["sum3_%d" % w], 32)
+        g.sync.dma_start(T.y3[w * rows:(w + 1) * rows, :], T.l3[4 * w:4 * w + 4]).then_inc(T.sem.st, 16)
+    g.wait_ge(T.sem.sent, sent)
+    g.wait_ge(T.sem.st, 16 * (3 + W3))
+
+
+def run_reducer(g, core, T, topo):
+    k = RED.index(core)
+    mine = [j for j in range(KS) if j % 4 == k]
+    g.wait_ge(T.sem.arrs, 4 * len(mine))
+    sent = fold(g, T, topo, core, [([T.rs[r * JS + i] for r in range(4)], T.ls[j]) for i, j in enumerate(mine)], 2,
+                T.sem.sums)
+    for w in range(W3):
+        g.wait_ge(T.sem["arr3_%d" % w], 16)
+        sent += fold(g, T, topo, core, [([T.r3[r * W3 + w] for r in range(4)], T.l3[4 * w + k])], 8,
+                     T.sem["sum3_%d" % w])
+    g.wait_ge(T.sem.sent, sent)
+
+
+def rank_program(g, core, T, topo):
+    rank = T.rank_of(core)
+    if rank is not None:
+        run_rank(g, core, T, topo, rank)
+    elif core in RED:
+        run_reducer(g, core, T, topo)

@@ -1,23 +1,27 @@
 from concourse.bass import DstId, RemoteDMATransfer
 
-W3 = 2
-N3 = 256 // W3
-NS = 32
-KS = 11
 RED = [3, 7, 11, 15]
-JS = 3
 
-SCRATCH = {
-    "p3": ("dram", [4 * W3, 128, N3], "float32"),
-    "ps": ("dram", [KS, 128, NS], "float32"),
-    "r3": ("dram", [4 * W3, 128, N3], "float32"),
-    "rs": ("dram", [4 * JS, 128, NS], "float32"),
-    "l3": ("dram", [4 * W3, 128, N3], "float32"),
-    "ls": ("dram", [KS, 128, NS], "float32"),
-}
-SEMAPHORES = (["lds", "arrs", "sums", "sent", "st"]
-              + ["ld3_%d" % w for w in range(W3)] + ["arr3_%d" % w for w in range(W3)]
-              + ["sum3_%d" % w for w in range(W3)])
+
+def x3_wave(name, r0, r1, queue):
+    return dict(name=name, K=4, n=2 * (r1 - r0), per1=4, per2=8,
+                parts=[((slice(0, 4),), "3", (slice(r0, r1), slice(None)), True, queue)])
+
+
+SMALL = dict(name="s", K=11, n=32, per1=1, per2=2,
+             parts=[((slice(0, 8),), "1", (slice(None),), True, "sync"),
+                    ((slice(8, 10),), "4", (slice(None),), True, "scalar"),
+                    ((10, slice(0, 4), slice(None)), "2", (slice(None), 0), True, "sync"),
+                    ((10, slice(4, 128), slice(None)), "4", (slice(0, 62), slice(None)), False, "scalar")])
+WAVES = [x3_wave("a", 0, 64, "sync"), x3_wave("b", 64, 128, "scalar"), SMALL]
+
+SCRATCH = {}
+SEMAPHORES = ["sent", "st"]
+for _w in WAVES:
+    SCRATCH["p" + _w["name"]] = ("dram", [_w["K"], 128, _w["n"]], "float32")
+    SCRATCH["r" + _w["name"]] = ("dram", [4 * ((_w["K"] + 3) // 4), 128, _w["n"]], "float32")
+    SCRATCH["l" + _w["name"]] = ("dram", [_w["K"], 128, _w["n"]], "float32")
+    SEMAPHORES += [p + _w["name"] for p in ("ld", "arr", "sum")]
 
 
 def bits(first, count):
@@ -29,66 +33,55 @@ def dst_id(topo, c):
     return DstId(rid=rid, pnc=pid)
 
 
-def send(g, T, topo, core, items, per, sem):
-    nxt = {True: 0, False: 8}
-    trs = []
-    for src, red, dst in items:
-        off = topo.chip(red) != topo.chip(core)
-        trs.append(RemoteDMATransfer(dst_ids=[dst_id(topo, red)], dma_engine_mask=bits(nxt[off], per),
-                                     remote_sem=sem, src=src, dst=dst))
-        nxt[off] += per
-    g.remote_dma_fused(trs, local_sem=T.sem.sent)
-    return per * len(trs)
-
-
-def fold(g, T, topo, core, items, per, sem):
-    far = [c for c in T.cores if topo.chip(c) != topo.chip(core)]
-    near = [c for c in T.cores if topo.chip(c) == topo.chip(core)]
-    trs = []
-    for i, (srcs, dst) in enumerate(items):
-        for base, group in ((0, far), (8, near)):
-            trs.append(RemoteDMATransfer(dst_ids=[dst_id(topo, c) for c in group],
-                                         dma_engine_mask=bits(base + i * per, per), remote_sem=sem,
-                                         srcs=srcs, dsts=[dst for c in group], alu_op=1))
-    g.remote_dma_fused(trs, local_sem=T.sem.sent)
-    return per * len(trs)
-
-
 def run_rank(g, core, T, topo, rank):
-    rows = 128 // W3
-    g.scalar.dma_start(T.ps[0:8], T.x1[:]).then_inc(T.sem.lds, 16)
-    g.scalar.dma_start(T.ps[8:10], T.x4[:]).then_inc(T.sem.lds, 16)
-    g.scalar.dma_start(T.ps[10, 0:4, :], T.x2[:, 0]).then_inc(T.sem.lds, 16)
-    g.scalar.dma_start(T.ps[10, 4:128, :], T.x4[0:62, :]).then_inc(T.sem.lds, 16)
-    for w in range(W3):
-        g.sync.dma_start(T.p3[4 * w:4 * w + 4], T.x3[w * rows:(w + 1) * rows, :]).then_inc(T.sem["ld3_%d" % w], 16)
-    g.wait_ge(T.sem.lds, 64)
-    sent = send(g, T, topo, core, [(T.ps[j], RED[j % 4], T.rs[rank * JS + j // 4]) for j in range(KS)], 1, T.sem.arrs)
-    for w in range(W3):
-        g.wait_ge(T.sem["ld3_%d" % w], 16)
-        sent += send(g, T, topo, core, [(T.p3[4 * w + k], RED[k], T.r3[rank * W3 + w]) for k in range(4)], 4,
-                     T.sem["arr3_%d" % w])
-    g.scalar.wait_ge(T.sem.sums, 2 * KS)
-    g.scalar.dma_start(T.y1[:], T.ls[0:8]).then_inc(T.sem.st, 16)
-    g.scalar.dma_start(T.y4[:], T.ls[8:10]).then_inc(T.sem.st, 16)
-    g.scalar.dma_start(T.y2[:, 0], T.ls[10, 0:4, :]).then_inc(T.sem.st, 16)
-    for w in range(W3):
-        g.sync.wait_ge(T.sem["sum3_%d" % w], 32)
-        g.sync.dma_start(T.y3[w * rows:(w + 1) * rows, :], T.l3[4 * w:4 * w + 4]).then_inc(T.sem.st, 16)
+    qs = {"sync": g.sync, "scalar": g.scalar}
+    for w in WAVES:
+        for at, t, idx, keep, q in w["parts"]:
+            qs[q].dma_start(T["p" + w["name"]][at], T["x" + t][idx]).then_inc(T.sem["ld" + w["name"]], 16)
+    sent = 0
+    for w in WAVES:
+        g.wait_ge(T.sem["ld" + w["name"]], 16 * len(w["parts"]))
+        nxt = {True: 0, False: 8}
+        trs = []
+        for j in range(w["K"]):
+            off = topo.chip(RED[j % 4]) != topo.chip(core)
+            trs.append(RemoteDMATransfer(dst_ids=[dst_id(topo, RED[j % 4])],
+                                         dma_engine_mask=bits(nxt[off], w["per1"]), remote_sem=T.sem["arr" + w["name"]],
+                                         src=T["p" + w["name"]][j],
+                                         dst=T["r" + w["name"]][rank * ((w["K"] + 3) // 4) + j // 4]))
+            nxt[off] += w["per1"]
+        g.remote_dma_fused(trs, local_sem=T.sem.sent)
+        sent += w["per1"] * len(trs)
+    stores = 0
+    for w in WAVES:
+        for q in sorted(set(p[4] for p in w["parts"] if p[3])):
+            qs[q].wait_ge(T.sem["sum" + w["name"]], w["per2"] * w["K"])
+        for at, t, idx, keep, q in w["parts"]:
+            if keep:
+                qs[q].dma_start(T["y" + t][idx], T["l" + w["name"]][at]).then_inc(T.sem.st, 16)
+                stores += 1
     g.wait_ge(T.sem.sent, sent)
-    g.wait_ge(T.sem.st, 16 * (3 + W3))
+    g.wait_ge(T.sem.st, 16 * stores)
 
 
 def run_reducer(g, core, T, topo):
     k = RED.index(core)
-    mine = [j for j in range(KS) if j % 4 == k]
-    g.wait_ge(T.sem.arrs, 4 * len(mine))
-    sent = fold(g, T, topo, core, [([T.rs[r * JS + i] for r in range(4)], T.ls[j]) for i, j in enumerate(mine)], 2,
-                T.sem.sums)
-    for w in range(W3):
-        g.wait_ge(T.sem["arr3_%d" % w], 16)
-        sent += fold(g, T, topo, core, [([T.r3[r * W3 + w] for r in range(4)], T.l3[4 * w + k])], 8,
-                     T.sem["sum3_%d" % w])
+    far = [c for c in T.cores if topo.chip(c) != topo.chip(core)]
+    near = [c for c in T.cores if topo.chip(c) == topo.chip(core)]
+    sent = 0
+    for w in WAVES:
+        mine = [j for j in range(w["K"]) if j % 4 == k]
+        g.wait_ge(T.sem["arr" + w["name"]], 4 * w["per1"] * len(mine))
+        trs = []
+        for i, j in enumerate(mine):
+            srcs = [T["r" + w["name"]][r * ((w["K"] + 3) // 4) + i] for r in range(4)]
+            for base, group in ((0, far), (8, near)):
+                trs.append(RemoteDMATransfer(dst_ids=[dst_id(topo, c) for c in group],
+                                             dma_engine_mask=bits(base + i * w["per2"], w["per2"]),
+                                             remote_sem=T.sem["sum" + w["name"]], srcs=srcs,
+                                             dsts=[T["l" + w["name"]][j] for c in group], alu_op=1))
+        g.remote_dma_fused(trs, local_sem=T.sem.sent)
+        sent += w["per2"] * len(trs)
     g.wait_ge(T.sem.sent, sent)
 
 

@@ -1,19 +1,15 @@
 from concourse.bass import DstId, RemoteDMATransfer
 
-RED = [3, 7, 11, 15]
+RED = [1, 3, 5, 7]
+ALL = slice(None)
 
-
-def x3_wave(name, r0, r1, queue):
-    return dict(name=name, K=4, n=2 * (r1 - r0), per1=4, per2=8,
-                parts=[((slice(0, 4),), "3", (slice(r0, r1), slice(None)), True, queue)])
-
-
-SMALL = dict(name="s", K=11, n=32, per1=1, per2=2,
-             parts=[((slice(0, 8),), "1", (slice(None),), True, "sync"),
-                    ((slice(8, 10),), "4", (slice(None),), True, "scalar"),
-                    ((10, slice(0, 4), slice(None)), "2", (slice(None), 0), True, "sync"),
-                    ((10, slice(4, 128), slice(None)), "4", (slice(0, 62), slice(None)), False, "scalar")])
-WAVES = [x3_wave("a", 0, 64, "sync"), x3_wave("b", 64, 128, "scalar"), SMALL]
+WAVES = [
+    dict(name="a", K=4, n=128, cap=16, parts=[((slice(0, 4),), "3", (slice(0, 64), ALL), "sync")]),
+    dict(name="b", K=4, n=128, cap=16, parts=[((slice(0, 4),), "3", (slice(64, 128), ALL), "scalar")]),
+    dict(name="s", K=5, n=64, cap=16, parts=[((slice(0, 4),), "1", (ALL,), "sync"),
+                                            ((4,), "4", (ALL,), "scalar")]),
+    dict(name="t", K=1, n=1, cap=1, parts=[((0, ALL, 0), "2", (ALL, 0), "scalar")]),
+]
 
 SCRATCH = {}
 SEMAPHORES = ["sent", "st"]
@@ -28,60 +24,66 @@ def bits(first, count):
     return ((1 << count) - 1) << first
 
 
+def share(w, engines, m):
+    return min(w["cap"], 1 << ((engines // m).bit_length() - 1))
+
+
 def dst_id(topo, c):
     rid, pid, _ = topo.addr(c)
     return DstId(rid=rid, pnc=pid)
 
 
+def mine_of(w, k):
+    return [j for j in range(w["K"]) if j % 4 == k]
+
+
 def run_rank(g, core, T, topo, rank):
     qs = {"sync": g.sync, "scalar": g.scalar}
+    here = topo.chip(core)
     for w in WAVES:
-        for at, t, idx, keep, q in w["parts"]:
+        for at, t, idx, q in w["parts"]:
             qs[q].dma_start(T["p" + w["name"]][at], T["x" + t][idx]).then_inc(T.sem["ld" + w["name"]], 16)
     sent = 0
     for w in WAVES:
         g.wait_ge(T.sem["ld" + w["name"]], 16 * len(w["parts"]))
-        nxt = {True: 0, False: 8}
+        per = share(w, 8, w["K"])
         trs = []
         for j in range(w["K"]):
-            off = topo.chip(RED[j % 4]) != topo.chip(core)
-            trs.append(RemoteDMATransfer(dst_ids=[dst_id(topo, RED[j % 4])],
-                                         dma_engine_mask=bits(nxt[off], w["per1"]), remote_sem=T.sem["arr" + w["name"]],
-                                         src=T["p" + w["name"]][j],
-                                         dst=T["r" + w["name"]][rank * ((w["K"] + 3) // 4) + j // 4]))
-            nxt[off] += w["per1"]
+            for base, ch in ((0, 1 - here), (8, here)):
+                trs.append(RemoteDMATransfer(dst_ids=[dst_id(topo, 8 * ch + RED[j % 4])],
+                                             dma_engine_mask=bits(base + j * per, per),
+                                             remote_sem=T.sem["arr" + w["name"]], src=T["p" + w["name"]][j],
+                                             dst=T["r" + w["name"]][rank * ((w["K"] + 3) // 4) + j // 4]))
         g.remote_dma_fused(trs, local_sem=T.sem.sent)
-        sent += w["per1"] * len(trs)
+        sent += per * len(trs)
     stores = 0
     for w in WAVES:
-        for q in sorted(set(p[4] for p in w["parts"] if p[3])):
-            qs[q].wait_ge(T.sem["sum" + w["name"]], w["per2"] * w["K"])
-        for at, t, idx, keep, q in w["parts"]:
-            if keep:
-                qs[q].dma_start(T["y" + t][idx], T["l" + w["name"]][at]).then_inc(T.sem.st, 16)
-                stores += 1
+        total = sum(len(mine_of(w, k)) * share(w, 16, len(mine_of(w, k))) for k in range(4) if mine_of(w, k))
+        for q in sorted(set(p[3] for p in w["parts"])):
+            qs[q].wait_ge(T.sem["sum" + w["name"]], total)
+        for at, t, idx, q in w["parts"]:
+            qs[q].dma_start(T["y" + t][idx], T["l" + w["name"]][at]).then_inc(T.sem.st, 16)
+            stores += 1
     g.wait_ge(T.sem.sent, sent)
     g.wait_ge(T.sem.st, 16 * stores)
 
 
 def run_reducer(g, core, T, topo):
-    k = RED.index(core)
-    far = [c for c in T.cores if topo.chip(c) != topo.chip(core)]
+    k = RED.index(core % 8)
     near = [c for c in T.cores if topo.chip(c) == topo.chip(core)]
     sent = 0
     for w in WAVES:
-        mine = [j for j in range(w["K"]) if j % 4 == k]
-        g.wait_ge(T.sem["arr" + w["name"]], 4 * w["per1"] * len(mine))
-        trs = []
-        for i, j in enumerate(mine):
-            srcs = [T["r" + w["name"]][r * ((w["K"] + 3) // 4) + i] for r in range(4)]
-            for base, group in ((0, far), (8, near)):
-                trs.append(RemoteDMATransfer(dst_ids=[dst_id(topo, c) for c in group],
-                                             dma_engine_mask=bits(base + i * w["per2"], w["per2"]),
-                                             remote_sem=T.sem["sum" + w["name"]], srcs=srcs,
-                                             dsts=[T["l" + w["name"]][j] for c in group], alu_op=1))
+        mine = mine_of(w, k)
+        if not mine:
+            continue
+        per = share(w, 16, len(mine))
+        g.wait_ge(T.sem["arr" + w["name"]], 4 * share(w, 8, w["K"]) * len(mine))
+        trs = [RemoteDMATransfer(dst_ids=[dst_id(topo, c) for c in near], dma_engine_mask=bits(i * per, per),
+                                 remote_sem=T.sem["sum" + w["name"]],
+                                 srcs=[T["r" + w["name"]][r * ((w["K"] + 3) // 4) + j // 4] for r in range(4)],
+                                 dsts=[T["l" + w["name"]][j] for c in near], alu_op=1) for i, j in enumerate(mine)]
         g.remote_dma_fused(trs, local_sem=T.sem.sent)
-        sent += w["per2"] * len(trs)
+        sent += per * len(trs)
     g.wait_ge(T.sem.sent, sent)
 
 
@@ -89,5 +91,5 @@ def rank_program(g, core, T, topo):
     rank = T.rank_of(core)
     if rank is not None:
         run_rank(g, core, T, topo, rank)
-    elif core in RED:
+    elif core % 8 in RED:
         run_reducer(g, core, T, topo)

from concourse.bass import DstId, RemoteDMATransfer

RED = [1, 3, 5, 7]
ALL = slice(None)

WAVES = [
    dict(name="a", K=4, n=128, cap=16, parts=[((slice(0, 4),), "3", (slice(0, 64), ALL), "sync")]),
    dict(name="b", K=4, n=128, cap=16, parts=[((slice(0, 4),), "3", (slice(64, 128), ALL), "scalar")]),
    dict(name="s", K=5, n=64, cap=16, parts=[((slice(0, 4),), "1", (ALL,), "sync"),
                                            ((4,), "4", (ALL,), "scalar")]),
    dict(name="t", K=1, n=1, cap=1, parts=[((0, ALL, 0), "2", (ALL, 0), "scalar")]),
]

SCRATCH = {}
SEMAPHORES = ["sent", "st"]
for _w in WAVES:
    SCRATCH["p" + _w["name"]] = ("dram", [_w["K"], 128, _w["n"]], "float32")
    SCRATCH["r" + _w["name"]] = ("dram", [4 * ((_w["K"] + 3) // 4), 128, _w["n"]], "float32")
    SCRATCH["l" + _w["name"]] = ("dram", [_w["K"], 128, _w["n"]], "float32")
    SEMAPHORES += [p + _w["name"] for p in ("ld", "arr", "sum")]


def bits(first, count):
    return ((1 << count) - 1) << first


def share(w, engines, m):
    return min(w["cap"], 1 << ((engines // m).bit_length() - 1))


def dst_id(topo, c):
    rid, pid, _ = topo.addr(c)
    return DstId(rid=rid, pnc=pid)


def mine_of(w, k):
    return [j for j in range(w["K"]) if j % 4 == k]


def run_rank(g, core, T, topo, rank):
    qs = {"sync": g.sync, "scalar": g.scalar}
    here = topo.chip(core)
    for w in WAVES:
        for at, t, idx, q in w["parts"]:
            qs[q].dma_start(T["p" + w["name"]][at], T["x" + t][idx]).then_inc(T.sem["ld" + w["name"]], 16)
    sent = 0
    for w in WAVES:
        g.wait_ge(T.sem["ld" + w["name"]], 16 * len(w["parts"]))
        per = share(w, 8, w["K"])
        trs = []
        for j in range(w["K"]):
            for base, ch in ((0, 1 - here), (8, here)):
                trs.append(RemoteDMATransfer(dst_ids=[dst_id(topo, 8 * ch + RED[j % 4])],
                                             dma_engine_mask=bits(base + j * per, per),
                                             remote_sem=T.sem["arr" + w["name"]], src=T["p" + w["name"]][j],
                                             dst=T["r" + w["name"]][rank * ((w["K"] + 3) // 4) + j // 4]))
        g.remote_dma_fused(trs, local_sem=T.sem.sent)
        sent += per * len(trs)
    stores = 0
    for w in WAVES:
        total = sum(len(mine_of(w, k)) * share(w, 16, len(mine_of(w, k))) for k in range(4) if mine_of(w, k))
        for q in sorted(set(p[3] for p in w["parts"])):
            qs[q].wait_ge(T.sem["sum" + w["name"]], total)
        for at, t, idx, q in w["parts"]:
            qs[q].dma_start(T["y" + t][idx], T["l" + w["name"]][at]).then_inc(T.sem.st, 16)
            stores += 1
    g.wait_ge(T.sem.sent, sent)
    g.wait_ge(T.sem.st, 16 * stores)


def run_reducer(g, core, T, topo):
    k = RED.index(core % 8)
    near = [c for c in T.cores if topo.chip(c) == topo.chip(core)]
    sent = 0
    for w in WAVES:
        mine = mine_of(w, k)
        if not mine:
            continue
        per = share(w, 16, len(mine))
        g.wait_ge(T.sem["arr" + w["name"]], 4 * share(w, 8, w["K"]) * len(mine))
        trs = [RemoteDMATransfer(dst_ids=[dst_id(topo, c) for c in near], dma_engine_mask=bits(i * per, per),
                                 remote_sem=T.sem["sum" + w["name"]],
                                 srcs=[T["r" + w["name"]][r * ((w["K"] + 3) // 4) + j // 4] for r in range(4)],
                                 dsts=[T["l" + w["name"]][j] for c in near], alu_op=1) for i, j in enumerate(mine)]
        g.remote_dma_fused(trs, local_sem=T.sem.sent)
        sent += per * len(trs)
    g.wait_ge(T.sem.sent, sent)


def rank_program(g, core, T, topo):
    rank = T.rank_of(core)
    if rank is not None:
        run_rank(g, core, T, topo, rank)
    elif core % 8 in RED:
        run_reducer(g, core, T, topo)
